import numpy as np
import ml_dtypes


def mxq(x, axis, fmt="e4m3"):
    dtype, down = {"e4m3": (ml_dtypes.float8_e4m3fn, 7), "e5m2": (ml_dtypes.float8_e5m2, 14)}[fmt]
    v = np.moveaxis(np.asarray(x, np.float32).astype(ml_dtypes.bfloat16).astype(np.float64), axis, -1)
    blocks = v.reshape(v.shape[:-1] + (-1, 32))
    amax = np.abs(blocks).max(-1, keepdims=True)
    byte = np.maximum(np.where(amax > 0, np.frexp(amax)[1] - 1 + 127, 0) - down, 1)
    scale = np.exp2(byte - 127.0)
    codes = (blocks / scale).astype(np.float32).astype(dtype).astype(np.float64)
    return np.moveaxis((codes * scale).reshape(v.shape), -1, axis)


WIDE = False


def mx_kscale(k):
    if not WIDE:
        return np.ones(k)
    levels = np.array([10, -10, 5, -5, 0])
    if k % 512:
        return np.exp2(np.random.permutation(np.resize(levels, k // 32))).repeat(32)
    a = np.empty((k // 512, 16))
    for p in range(k // 512):
        a[p, :8] = np.random.permutation(np.resize(levels, 8))
        for g in range(8):
            far = levels[np.abs(levels - a[p, g]) >= 10]
            a[p, g + 8] = far[np.random.randint(len(far))]
    return np.exp2(a.ravel()).repeat(32)


BF16 = ml_dtypes.bfloat16


def bf(x):
    return np.asarray(x, np.float32).astype(BF16)


def f64(x):
    return np.asarray(x).astype(np.float64)


B, V, H = 8192, 256, 512


def draw0():
    c = mx_kscale(H)
    t = mx_kscale(B)
    u = mx_kscale(B)
    return {"v": bf(np.random.uniform(-1.0, 1.0, (B, V)) * u[:, None]),
            "hp": bf(np.random.uniform(-1.0, 1.0, (B, H)) / u[:, None]),
            "hf": bf(np.random.uniform(-1.0, 1.0, (B, H)) * c),
            "hn": bf(np.random.uniform(-1.0, 1.0, (B, H)) / t[:, None]),
            "w": bf(np.random.standard_normal((V, H)) * 2.0 / np.sqrt(H) / c),
            "b": bf(0.3 * np.random.standard_normal(V)),
            "s": bf((1.0 + 0.1 * np.random.standard_normal(B)) * t)}


def visible_mean_field(h, w, b):
    return np.tanh((mxq(h, 1, "e4m3") @ mxq(w, 1, "e4m3").T) + b)


def correlation(vis, hid):
    return mxq(vis, 0, "e4m3").T @ mxq(hid, 0, "e4m3")


def core(v, hp, hf, hn, w, b, s):
    n_rows = v.shape[0]
    v1 = visible_mean_field(f64(hf), f64(w), f64(b))
    v1s = f64(s)[:, None] * v1
    neg = correlation(v1s, f64(hn))
    pos = correlation(f64(v), f64(hp))
    g = (pos - neg) / np.sqrt(n_rows)
    return g


def e4m3fn_bytes(y):
    return np.clip(np.asarray(y, np.float64), -448.0, 448.0).astype(np.float32).astype(ml_dtypes.float8_e4m3fn).view(np.uint8)


def e4m3fn_values(b):
    return np.asarray(b, np.uint8).view(ml_dtypes.float8_e4m3fn).astype(np.float64)


def setup_inputs():
    d = draw0()
    x0 = np.asarray(d['hp']).astype(np.float64)
    s = (np.max(np.abs(x0), axis=(1,), keepdims=True) / 448.0).astype(np.float32)
    out = {}
    for k, v in d.items():
        if k == 'hp':
            out['hp_bytes'] = e4m3fn_bytes(x0 / s.astype(np.float64))
            out['hp_scale'] = s
        else:
            out[k] = v
    return out


def reference(v, hp_bytes, hp_scale, hf, hn, w, b, s):
    return core(v, e4m3fn_values(hp_bytes) * hp_scale.astype(np.float64), hf, hn, w, b, s)

@@ -1,0 +1,315 @@
+from contextlib import ExitStack
+
+import concourse.mybir as mybir
+from concourse.masks import make_identity
+
+F32 = mybir.dt.float32
+BF16 = mybir.dt.bfloat16
+U32 = mybir.dt.uint32
+U8 = mybir.dt.uint8
+FP8 = mybir.dt.float8_e4m3fn
+FP8X4 = mybir.dt.float8_e4m3fn_x4
+ACT = mybir.ActivationFunctionType
+ALU = mybir.AluOpType
+
+B, V, H = 8192, 256, 512
+P = 128
+T = 4
+ROWS = P * T
+CHUNKS = B // ROWS
+M_TILES = V // P
+CHAIN_LAG = 2
+STEPS = CHUNKS + CHAIN_LAG
+LEAD = 2
+
+FLOPS = 3 * 2 * B * V * H
+
+
+HN_GAPS = (3, 8)
+HP_GAPS = (4, 9)
+
+
+def chunk_of_step(step, gaps):
+    if step < 0 or step in gaps:
+        return None
+    chunk = step - sum(1 for gap in gaps if gap < step)
+    return chunk if chunk < CHUNKS else None
+
+
+def interleave(copy, dst, src, n):
+    copy(
+        out=dst.rearrange("p (c i t) -> p c t i", i=4, t=T),
+        in_=src.rearrange("p t (c i) -> p c t i", i=4),
+    )
+
+
+def tile_persistentmeanfieldisingrbmgradient_t_kernel(tc, v, hp_bytes, hp_scale, hf, hn, w, b, s, out):
+    nc = tc.nc
+
+    v_rows = v.rearrange("(g p t) n -> g p t n", p=P, t=T)
+    hp_rows = hp_bytes.rearrange("(g p t) n -> g p t n", p=P, t=T)
+    hf_rows = hf.rearrange("(g p t) n -> g p t n", p=P, t=T)
+    hn_rows = hn.rearrange("(g p t) n -> g p t n", p=P, t=T)
+
+    with ExitStack() as ctx:
+        keep = ctx.enter_context(tc.tile_pool(name="keep", bufs=1))
+        loads = ctx.enter_context(tc.tile_pool(name="loads", bufs=4))
+        work = ctx.enter_context(tc.tile_pool(name="work", bufs=2))
+        codes = ctx.enter_context(tc.tile_pool(name="codes", bufs=3))
+        psum = ctx.enter_context(tc.psum_pool(name="psum", bufs=1))
+        ctx.enter_context(tc.manual_schedule())
+
+        warm = keep.tile([P, 1], F32, name="warm")
+        nc.vector.memset(warm[:], 0.0)
+        nc.scalar.activation(out=warm[:], in_=warm[:], func=ACT.Tanh)
+        scale_rows = keep.tile([P, ROWS], F32, name="scale_rows")
+        nc.vector.memset(scale_rows[:], 0.0)
+        vec_rows = keep.tile([P, ROWS], BF16, name="vec_rows")
+        nc.gpsimd.memset(vec_rows[:], 0.0)
+        ident = keep.tile([P, P], F32, name="ident")
+        make_identity(nc, ident[:])
+
+        hf_raw, hn_raw, hp_raw, v_raw = {}, {}, {}, {}
+
+        def load(store, name, rows, chunk, width, dtype):
+            tile = loads.tile([P, T, width], dtype, name=name, tag=name)
+            nc.sync.dma_start(out=tile[:], in_=rows[chunk])
+            store[chunk] = tile
+
+        def load_hp(c):
+            load(hp_raw, "hp_raw", hp_rows, c, H, U8)
+
+        def load_v(c):
+            load(v_raw, "v_raw", v_rows, c, V, BF16)
+
+        def load_hn(c):
+            load(hn_raw, "hn_raw", hn_rows, c, H, BF16)
+
+        def load_hf(c):
+            load(hf_raw, "hf_raw", hf_rows, c, H, BF16)
+
+        load_v(0)
+        nc.scalar.dma_start(out=scale_rows[0:CHUNKS, :], in_=hp_scale.rearrange("(g x) o -> g (x o)", x=ROWS))
+        nc.scalar.dma_start(out=vec_rows[0:CHUNKS, :], in_=s.rearrange("(g x) -> g x", x=ROWS))
+        nc.scalar.dma_start(out=vec_rows[32 : 32 + M_TILES, 0:P], in_=b.rearrange("(m x) -> m x", x=P))
+        load_hn(0)
+        load_hp(0)
+        load_hf(0)
+        w_raw = keep.tile([P, M_TILES, H], BF16, name="w_raw")
+        nc.sync.dma_start(out=w_raw[:], in_=w.rearrange("(m p) k -> p m k", p=P))
+        load_hf(1)
+        load_hp(1)
+        load_v(1)
+        load_hn(1)
+        load_hf(2)
+
+        neg_s = keep.tile([P, T, CHUNKS], F32, name="neg_s")
+        hp_sc = keep.tile([P, T, CHUNKS], F32, name="hp_sc")
+        b_col = keep.tile([P, M_TILES], F32, name="b_col")
+        w_codes = keep.tile([P, V], U32, name="w_codes", align_bytes=64)
+        w_scales = keep.tile([P, V], U8, name="w_scales", align_bytes=64)
+
+        acc = [psum.tile([P, H], F32, name="acc%d" % m, tag="acc%d" % m) for m in range(M_TILES)]
+        acc_passes = [0, 0]
+
+        hf_turned, hf_codes, field, mean, mean_turned, v1_group, v1_codes = {}, {}, {}, {}, {}, {}, {}
+        hp_bf, v_group, v_codes, hn_group, hp_group, hn_codes, hp_codes = {}, {}, {}, {}, {}, {}, {}
+
+        def turn_words(words, name):
+            bank = psum.tile([P, 2, 2, P], F32, name=name, tag=name)
+            for r in range(2):
+                for u in range(2):
+                    nc.tensor.transpose(bank[:, r, u, :], words[:, 256 * r + u : 256 * (r + 1) : 2], ident[:])
+            return bank
+
+        def empty_turned(copy, bank, dst):
+            copy(
+                out=dst.bitcast(F32).rearrange("p (r c u) -> p r c u", r=2, u=2),
+                in_=bank[:].rearrange("p r u c -> p r c u"),
+            )
+
+        def turn_hf(c):
+            words = hf_raw[c][:].rearrange("p t h -> p (t h)").bitcast(F32)
+            hf_turned[c] = [turn_words(words[:, 512 * i : 512 * (i + 1)], "turn%d" % i) for i in range(2)]
+
+        def empty_hf(c):
+            tile = work.tile([P, T * ROWS], BF16, name="hf_group", tag="hf_group", align_bytes=64)
+            for i in range(2):
+                empty_turned(nc.scalar.copy, hf_turned[c][i], tile[:, 1024 * i : 1024 * (i + 1)])
+            hf_turned[c] = tile
+
+        def quantize(src, width, name):
+            code = codes.tile([P, width], U32, name=name + "_codes", tag=name + "_codes", align_bytes=64)
+            scale = codes.tile([P, width], U8, name=name + "_scales", tag=name + "_scales", align_bytes=64)
+            nc.vector.quantize_mx(out=code[:].bitcast(FP8X4), scales=scale[:], in_=src[:])
+            return code, scale
+
+        def fields(c):
+            code, scale = hf_codes[c]
+            banks = []
+            for m in range(M_TILES):
+                bank = psum.tile([P, ROWS], F32, name="field%d" % m, tag="field%d" % m)
+                cols = slice(m * P, (m + 1) * P)
+                nc.tensor.matmul_mx(
+                    out=bank[:],
+                    lhsT=w_codes[:, cols].bitcast(FP8X4),
+                    lhsT_scale=w_scales[:, cols],
+                    rhs=code[:].bitcast(FP8X4),
+                    rhs_scale=scale[:],
+                    start=True,
+                    stop=True,
+                )
+                banks.append(bank)
+            field[c] = banks
+
+        def means(c):
+            tile = work.tile([P, M_TILES, ROWS], F32, name="mean", tag="mean")
+            for m in range(M_TILES):
+                nc.scalar.activation(
+                    out=tile[:, m, :], in_=field[c][m][:], func=ACT.Tanh, bias=b_col[:, m : m + 1], scale=1.0
+                )
+            mean[c] = tile
+
+        def turn_means(c):
+            banks = []
+            for m in range(M_TILES):
+                bank = psum.tile([P, T, P], F32, name="back%d" % m, tag="back%d" % m)
+                for t in range(T):
+                    nc.tensor.transpose(bank[:, t, :], mean[c][:, m, t * P : (t + 1) * P], ident[:])
+                banks.append(bank)
+            mean_turned[c] = banks
+
+        def weigh_means(c):
+            tile = work.tile([P, V * T], BF16, name="v1_group", tag="v1_group", align_bytes=64)
+            for m in range(M_TILES):
+                nc.vector.tensor_tensor(
+                    out=tile[:, m * P * T : (m + 1) * P * T].rearrange("p (n t) -> p n t", t=T),
+                    in0=mean_turned[c][m][:].rearrange("p t n -> p n t"),
+                    in1=neg_s[:, :, c].unsqueeze(1).to_broadcast([P, P, T]),
+                    op=ALU.mult,
+                )
+            v1_group[c] = tile
+
+        def widen_hp(c):
+            tile = work.tile([P, T, H], BF16, name="hp_bf", tag="hp_bf")
+            for t in range(T):
+                nc.scalar.activation(
+                    out=tile[:, t, :], in_=hp_raw[c][:, t, :].bitcast(FP8), func=ACT.Copy, scale=hp_sc[:, t, c : c + 1]
+                )
+            hp_bf[c] = tile
+
+        def group_v(c):
+            tile = work.tile([P, V * T], BF16, name="v_group", tag="v_group", align_bytes=64)
+            interleave(nc.scalar.copy, tile[:], v_raw[c][:], V)
+            v_group[c] = tile
+
+        def group_h(copy, src, name):
+            tile = work.tile([P, H * T], BF16, name=name, tag=name, align_bytes=64)
+            interleave(copy, tile[:], src[:], H)
+            return tile
+
+        def add_passes(lhs, rhs):
+            code, scale = lhs
+            rcode, rscale = rhs
+            for m in range(M_TILES):
+                cols = slice(m * P, (m + 1) * P)
+                nc.tensor.matmul_mx(
+                    out=acc[m][:],
+                    lhsT=code[:, cols].bitcast(FP8X4),
+                    lhsT_scale=scale[:, cols],
+                    rhs=rcode[:].bitcast(FP8X4),
+                    rhs_scale=rscale[:],
+                    start=(acc_passes[m] == 0),
+                    stop=(acc_passes[m] == 2 * CHUNKS - 1),
+                )
+                acc_passes[m] = acc_passes[m] + 1
+
+        scale_bank = psum.tile([P, T, P], F32, name="back0", tag="back0")
+        for t in range(T):
+            nc.tensor.transpose(scale_bank[:, t, :], scale_rows[:, t::T], ident[:])
+        group_v(0)
+        nc.scalar.copy(out=hp_sc[:], in_=scale_bank[:, :, 0:CHUNKS])
+        hn_group[0] = group_h(nc.vector.tensor_copy, hn_raw[0], "hn_group")
+        vec_f32 = keep.tile([P, ROWS], F32, name="vec_f32")
+        nc.vector.tensor_copy(out=vec_f32[:], in_=vec_rows[:])
+        s_bank = psum.tile([P, T, P], F32, name="back1", tag="back1")
+        for t in range(T):
+            nc.tensor.transpose(s_bank[:, t, :], vec_f32[:, t::T], ident[:])
+        b_bank = psum.tile([P, P], F32, name="field0", tag="field0")
+        nc.tensor.transpose(b_bank[:], vec_f32[:, 0:P], ident[:])
+        nc.vector.tensor_scalar(out=neg_s[:], in0=s_bank[:, :, 0:CHUNKS], scalar1=-1.0, scalar2=None, op0=ALU.mult)
+        nc.vector.tensor_copy(out=b_col[:], in_=b_bank[:, 32 : 32 + M_TILES])
+        widen_hp(0)
+        turn_hf(0)
+
+        for step in range(STEPS + 1):
+            hn_now = chunk_of_step(step, HN_GAPS)
+            hp_now = chunk_of_step(step, HP_GAPS)
+            hp_next = chunk_of_step(step + 1, HP_GAPS)
+            hp_prev = chunk_of_step(step - 1, HP_GAPS)
+            hn_next = chunk_of_step(step + 1, HN_GAPS)
+
+            for ahead in range(LEAD + 1):
+                c = chunk_of_step(step + ahead + 1, HP_GAPS)
+                if c is not None and c not in hp_raw:
+                    load_hp(c)
+                    load_v(c)
+                c = step + ahead + 1
+                if c < CHUNKS and c not in hf_raw:
+                    load_hf(c)
+                c = chunk_of_step(step + ahead + 1, HN_GAPS)
+                if c is not None and c not in hn_raw:
+                    load_hn(c)
+
+            if 0 <= step - 1 < CHUNKS:
+                fields(step - 1)
+            if hp_prev is not None:
+                add_passes(v_codes[hp_prev], hp_codes[hp_prev])
+
+            if step < CHUNKS:
+                empty_hf(step)
+            if 0 <= step - 1 < CHUNKS:
+                means(step - 1)
+
+            if 0 <= step - 2 < CHUNKS:
+                weigh_means(step - 2)
+
+            if step + 1 < CHUNKS:
+                turn_hf(step + 1)
+            if 0 <= step - 3 < CHUNKS:
+                add_passes(v1_codes[step - 3], hn_codes[step - 3])
+            if 0 <= step - 1 < CHUNKS:
+                turn_means(step - 1)
+
+            if hp_next is not None:
+                widen_hp(hp_next)
+                group_v(hp_next)
+            if hn_next == CHUNKS - 1:
+                hn_group[hn_next] = group_h(nc.scalar.copy, hn_raw[hn_next], "hn_group")
+
+            if hp_now is not None:
+                hp_group[hp_now] = group_h(nc.vector.tensor_copy, hp_bf[hp_now], "hp_group")
+            if 0 <= step - 2 < CHUNKS:
+                v1_codes[step - 2] = quantize(v1_group[step - 2], V, "v1")
+            if hn_now is not None:
+                hn_codes[hn_now] = quantize(hn_group[hn_now], H, "hn")
+            if hp_now is not None:
+                v_codes[hp_now] = quantize(v_group[hp_now], V, "v")
+                hp_codes[hp_now] = quantize(hp_group[hp_now], H, "hp")
+            if step == 0:
+                w_bank = turn_words(w_raw[:].rearrange("p m k -> p (m k)").bitcast(F32), "back0")
+                w_group = keep.tile([P, V * T], BF16, name="w_group", align_bytes=64)
+                empty_turned(nc.vector.tensor_copy, w_bank, w_group[:])
+                nc.vector.quantize_mx(out=w_codes[:].bitcast(FP8X4), scales=w_scales[:], in_=w_group[:])
+            if step < CHUNKS:
+                hf_codes[step] = quantize(hf_turned[step], ROWS, "hf")
+            if hn_next is not None and hn_next < CHUNKS - 1:
+                hn_group[hn_next] = group_h(nc.vector.tensor_copy, hn_raw[hn_next], "hn_group")
+
+        for m in range(M_TILES):
+            result = keep.tile([P, H], F32, name="result%d" % m)
+            if m == 0:
+                nc.scalar.activation(out=result[:], in_=acc[m][:], func=ACT.Copy, scale=B ** -0.5)
+            else:
+                nc.vector.tensor_scalar(out=result[:], in0=acc[m][:], scalar1=B ** -0.5, scalar2=None, op0=ALU.mult)
+            nc.sync.dma_start(out=out[m * P : (m + 1) * P, :], in_=result[:])

@@ -9,51 +9,41 @@ U32 = mybir.dt.uint32
 U8 = mybir.dt.uint8
 FP8 = mybir.dt.float8_e4m3fn
 FP8X4 = mybir.dt.float8_e4m3fn_x4
-ACT = mybir.ActivationFunctionType
-ALU = mybir.AluOpType
+TANH = mybir.ActivationFunctionType.Tanh
+COPY = mybir.ActivationFunctionType.Copy
+MULT = mybir.AluOpType.mult
+ADD = mybir.AluOpType.add
 
 B, V, H = 8192, 256, 512
 P = 128
 T = 4
 ROWS = P * T
 CHUNKS = B // ROWS
-M_TILES = V // P
-CHAIN_LAG = 2
-STEPS = CHUNKS + CHAIN_LAG
-LEAD = 2
+V_TILES = V // P
+B_ROW = 32
+
+LOADS_AHEAD = 3
+HN_PAUSE = 12
+
+V_ON_SCALAR = 224
+HN_ON_GPSIMD = 176
+LAST_HN_ON_SCALAR = 320
+LAST_HP_ON_SCALAR = 256
 
 FLOPS = 3 * 2 * B * V * H
 
 
-HN_GAPS = (3, 8)
-HP_GAPS = (4, 9)
-
-
-def chunk_of_step(step, gaps):
-    if step < 0 or step in gaps:
-        return None
-    chunk = step - sum(1 for gap in gaps if gap < step)
-    return chunk if chunk < CHUNKS else None
-
-
-def interleave(copy, dst, src, n):
-    copy(
-        out=dst.rearrange("p (c i t) -> p c t i", i=4, t=T),
-        in_=src.rearrange("p t (c i) -> p c t i", i=4),
-    )
+def hn_chunk(step):
+    chunk = step if step < HN_PAUSE else step - 1
+    return chunk if step != HN_PAUSE and chunk < CHUNKS else None
 
 
 def tile_persistentmeanfieldisingrbmgradient_t_kernel(tc, v, hp_bytes, hp_scale, hf, hn, w, b, s, out):
     nc = tc.nc
 
-    v_rows = v.rearrange("(g p t) n -> g p t n", p=P, t=T)
-    hp_rows = hp_bytes.rearrange("(g p t) n -> g p t n", p=P, t=T)
-    hf_rows = hf.rearrange("(g p t) n -> g p t n", p=P, t=T)
-    hn_rows = hn.rearrange("(g p t) n -> g p t n", p=P, t=T)
-
     with ExitStack() as ctx:
         keep = ctx.enter_context(tc.tile_pool(name="keep", bufs=1))
-        loads = ctx.enter_context(tc.tile_pool(name="loads", bufs=4))
+        raw = ctx.enter_context(tc.tile_pool(name="raw", bufs=4))
         work = ctx.enter_context(tc.tile_pool(name="work", bufs=2))
         codes = ctx.enter_context(tc.tile_pool(name="codes", bufs=3))
         psum = ctx.enter_context(tc.psum_pool(name="psum", bufs=1))
@@ -61,255 +51,292 @@ def tile_persistentmeanfieldisingrbmgradient_t_kernel(tc, v, hp_bytes, hp_scale,
 
         warm = keep.tile([P, 1], F32, name="warm")
         nc.vector.memset(warm[:], 0.0)
-        nc.scalar.activation(out=warm[:], in_=warm[:], func=ACT.Tanh)
+        nc.scalar.activation(out=warm[:], in_=warm[:], func=TANH)
         scale_rows = keep.tile([P, ROWS], F32, name="scale_rows")
         nc.vector.memset(scale_rows[:], 0.0)
-        vec_rows = keep.tile([P, ROWS], BF16, name="vec_rows")
-        nc.gpsimd.memset(vec_rows[:], 0.0)
+        vector_rows = keep.tile([P, ROWS], BF16, name="vector_rows")
+        nc.gpsimd.memset(vector_rows[:], 0.0)
         ident = keep.tile([P, P], F32, name="ident")
         make_identity(nc, ident[:])
 
-        hf_raw, hn_raw, hp_raw, v_raw = {}, {}, {}, {}
+        hp_raw, v_raw, hn_raw, hf_raw = {}, {}, {}, {}
 
-        def load(store, name, rows, chunk, width, dtype):
-            tile = loads.tile([P, T, width], dtype, name=name, tag=name)
-            nc.sync.dma_start(out=tile[:], in_=rows[chunk])
-            store[chunk] = tile
+        def load(store, name, source, chunk, dtype):
+            rows = source.rearrange("(g p t) n -> g p t n", p=P, t=T)[chunk]
+            store[chunk] = raw.tile([P, T, source.shape[1]], dtype, name=name, tag=name)
+            nc.sync.dma_start(out=store[chunk][:], in_=rows)
 
-        def load_hp(c):
-            load(hp_raw, "hp_raw", hp_rows, c, H, U8)
+        def load_hp(chunk):
+            load(hp_raw, "hp_raw", hp_bytes, chunk, U8)
 
-        def load_v(c):
-            load(v_raw, "v_raw", v_rows, c, V, BF16)
+        def load_v(chunk):
+            load(v_raw, "v_raw", v, chunk, BF16)
 
-        def load_hn(c):
-            load(hn_raw, "hn_raw", hn_rows, c, H, BF16)
+        def load_hn(chunk):
+            load(hn_raw, "hn_raw", hn, chunk, BF16)
 
-        def load_hf(c):
-            load(hf_raw, "hf_raw", hf_rows, c, H, BF16)
+        def load_hf(chunk):
+            load(hf_raw, "hf_raw", hf, chunk, BF16)
 
-        load_v(0)
         nc.scalar.dma_start(out=scale_rows[0:CHUNKS, :], in_=hp_scale.rearrange("(g x) o -> g (x o)", x=ROWS))
-        nc.scalar.dma_start(out=vec_rows[0:CHUNKS, :], in_=s.rearrange("(g x) -> g x", x=ROWS))
-        nc.scalar.dma_start(out=vec_rows[32 : 32 + M_TILES, 0:P], in_=b.rearrange("(m x) -> m x", x=P))
-        load_hn(0)
-        load_hp(0)
-        load_hf(0)
-        w_raw = keep.tile([P, M_TILES, H], BF16, name="w_raw")
-        nc.sync.dma_start(out=w_raw[:], in_=w.rearrange("(m p) k -> p m k", p=P))
-        load_hf(1)
-        load_hp(1)
-        load_v(1)
-        load_hn(1)
-        load_hf(2)
+        nc.scalar.dma_start(out=vector_rows[0:CHUNKS, :], in_=s.rearrange("(g x) -> g x", x=ROWS))
+        nc.scalar.dma_start(out=vector_rows[B_ROW : B_ROW + V_TILES, 0:P], in_=b.rearrange("(m x) -> m x", x=P))
+        w_raw = keep.tile([P, V_TILES, H], BF16, name="w_raw")
 
-        neg_s = keep.tile([P, T, CHUNKS], F32, name="neg_s")
-        hp_sc = keep.tile([P, T, CHUNKS], F32, name="hp_sc")
-        b_col = keep.tile([P, M_TILES], F32, name="b_col")
+        load_hp(0)
+        load_v(0)
+        load_hn(0)
+        nc.sync.dma_start(out=w_raw[:], in_=w.rearrange("(m p) k -> p m k", p=P))
+        load_hf(0)
+        load_hf(1)
+        load_v(1)
+        load_hp(1)
+        load_hf(2)
+        load_hn(1)
+        load_hp(2)
+        load_v(2)
+        load_hn(2)
+
+        hp_factor = keep.tile([P, T, CHUNKS], F32, name="hp_factor")
+        minus_s = keep.tile([P, T, CHUNKS], F32, name="minus_s")
+        bias = keep.tile([P, V_TILES], F32, name="bias")
         w_codes = keep.tile([P, V], U32, name="w_codes", align_bytes=64)
         w_scales = keep.tile([P, V], U8, name="w_scales", align_bytes=64)
+        total = [psum.tile([P, H], F32, name="total%d" % m, tag="total%d" % m) for m in range(V_TILES)]
+        passes = [0, 0]
 
-        acc = [psum.tile([P, H], F32, name="acc%d" % m, tag="acc%d" % m) for m in range(M_TILES)]
-        acc_passes = [0, 0]
+        hf_turned, hf_grouped, hf_mx, field, mean, mean_turned, v1_grouped, v1_mx = {}, {}, {}, {}, {}, {}, {}, {}
+        hp_wide, hp_grouped, hp_mx, v_grouped, v_mx, hn_grouped, hn_mx = {}, {}, {}, {}, {}, {}, {}
 
-        hf_turned, hf_codes, field, mean, mean_turned, v1_group, v1_codes = {}, {}, {}, {}, {}, {}, {}
-        hp_bf, v_group, v_codes, hn_group, hp_group, hn_codes, hp_codes = {}, {}, {}, {}, {}, {}, {}
+        def gpsimd_copy(out, in_):
+            nc.gpsimd.tensor_scalar(out=out, in0=in_, scalar1=1.0, scalar2=0.0, op0=MULT, op1=ADD)
 
-        def turn_words(words, name):
-            bank = psum.tile([P, 2, 2, P], F32, name=name, tag=name)
+        def interleave(copy, grouped, source, start, stop):
+            if start < stop:
+                copy(
+                    out=grouped[:, start * T : stop * T].rearrange("p (c i t) -> p c t i", i=4, t=T),
+                    in_=source[:, :, start:stop].rearrange("p t (c i) -> p c t i", i=4),
+                )
+
+        def grouped_tile(name, columns, bufs=2):
+            return work.tile([P, columns * T], BF16, name=name, tag=name, align_bytes=64, bufs=bufs)
+
+        def quantize(grouped, columns, name):
+            code = codes.tile([P, columns], U32, name=name + "_codes", tag=name + "_codes", align_bytes=64)
+            scale = codes.tile([P, columns], U8, name=name + "_scales", tag=name + "_scales", align_bytes=64)
+            nc.vector.quantize_mx(out=code[:].bitcast(FP8X4), scales=scale[:], in_=grouped[:])
+            return code, scale
+
+        def turn_two_rows(words, bank_name):
+            bank = psum.tile([P, 2, 2, P], F32, name=bank_name, tag=bank_name)
             for r in range(2):
                 for u in range(2):
                     nc.tensor.transpose(bank[:, r, u, :], words[:, 256 * r + u : 256 * (r + 1) : 2], ident[:])
             return bank
 
-        def empty_turned(copy, bank, dst):
+        def empty_turned(copy, bank, grouped):
             copy(
-                out=dst.bitcast(F32).rearrange("p (r c u) -> p r c u", r=2, u=2),
+                out=grouped.bitcast(F32).rearrange("p (r c u) -> p r c u", r=2, u=2),
                 in_=bank[:].rearrange("p r u c -> p r c u"),
             )
 
-        def turn_hf(c):
-            words = hf_raw[c][:].rearrange("p t h -> p (t h)").bitcast(F32)
-            hf_turned[c] = [turn_words(words[:, 512 * i : 512 * (i + 1)], "turn%d" % i) for i in range(2)]
+        def turn_hf(chunk):
+            words = hf_raw[chunk][:].rearrange("p t k -> p (t k)").bitcast(F32)
+            hf_turned[chunk] = [turn_two_rows(words[:, 512 * i : 512 * (i + 1)], "turned%d" % i) for i in range(2)]
 
-        def empty_hf(c):
-            tile = work.tile([P, T * ROWS], BF16, name="hf_group", tag="hf_group", align_bytes=64)
+        def empty_hf(chunk):
+            hf_grouped[chunk] = grouped_tile("hf_grouped", ROWS)
             for i in range(2):
-                empty_turned(nc.scalar.copy, hf_turned[c][i], tile[:, 1024 * i : 1024 * (i + 1)])
-            hf_turned[c] = tile
+                empty_turned(nc.scalar.copy, hf_turned[chunk][i], hf_grouped[chunk][:, 1024 * i : 1024 * (i + 1)])
 
-        def quantize(src, width, name):
-            code = codes.tile([P, width], U32, name=name + "_codes", tag=name + "_codes", align_bytes=64)
-            scale = codes.tile([P, width], U8, name=name + "_scales", tag=name + "_scales", align_bytes=64)
-            nc.vector.quantize_mx(out=code[:].bitcast(FP8X4), scales=scale[:], in_=src[:])
-            return code, scale
+        def quantize_hf(chunk):
+            hf_mx[chunk] = quantize(hf_grouped[chunk], ROWS, "hf")
 
-        def fields(c):
-            code, scale = hf_codes[c]
-            banks = []
-            for m in range(M_TILES):
+        def compute_fields(chunk):
+            code, scale = hf_mx[chunk]
+            field[chunk] = []
+            for m in range(V_TILES):
+                units = slice(m * P, (m + 1) * P)
                 bank = psum.tile([P, ROWS], F32, name="field%d" % m, tag="field%d" % m)
-                cols = slice(m * P, (m + 1) * P)
                 nc.tensor.matmul_mx(
                     out=bank[:],
-                    lhsT=w_codes[:, cols].bitcast(FP8X4),
-                    lhsT_scale=w_scales[:, cols],
+                    lhsT=w_codes[:, units].bitcast(FP8X4),
+                    lhsT_scale=w_scales[:, units],
                     rhs=code[:].bitcast(FP8X4),
                     rhs_scale=scale[:],
                     start=True,
                     stop=True,
                 )
-                banks.append(bank)
-            field[c] = banks
+                field[chunk].append(bank)
 
-        def means(c):
-            tile = work.tile([P, M_TILES, ROWS], F32, name="mean", tag="mean")
-            for m in range(M_TILES):
+        def compute_means(chunk):
+            mean[chunk] = work.tile([P, V_TILES, ROWS], F32, name="mean", tag="mean")
+            for m in range(V_TILES):
                 nc.scalar.activation(
-                    out=tile[:, m, :], in_=field[c][m][:], func=ACT.Tanh, bias=b_col[:, m : m + 1], scale=1.0
+                    out=mean[chunk][:, m, :], in_=field[chunk][m][:], func=TANH, bias=bias[:, m : m + 1], scale=1.0
                 )
-            mean[c] = tile
 
-        def turn_means(c):
-            banks = []
-            for m in range(M_TILES):
+        def turn_means(chunk):
+            mean_turned[chunk] = []
+            for m in range(V_TILES):
                 bank = psum.tile([P, T, P], F32, name="back%d" % m, tag="back%d" % m)
                 for t in range(T):
-                    nc.tensor.transpose(bank[:, t, :], mean[c][:, m, t * P : (t + 1) * P], ident[:])
-                banks.append(bank)
-            mean_turned[c] = banks
+                    nc.tensor.transpose(bank[:, t, :], mean[chunk][:, m, t * P : (t + 1) * P], ident[:])
+                mean_turned[chunk].append(bank)
 
-        def weigh_means(c):
-            tile = work.tile([P, V * T], BF16, name="v1_group", tag="v1_group", align_bytes=64)
-            for m in range(M_TILES):
+        def weigh_means(chunk):
+            v1_grouped[chunk] = grouped_tile("v1_grouped", V)
+            for m in range(V_TILES):
                 nc.vector.tensor_tensor(
-                    out=tile[:, m * P * T : (m + 1) * P * T].rearrange("p (n t) -> p n t", t=T),
-                    in0=mean_turned[c][m][:].rearrange("p t n -> p n t"),
-                    in1=neg_s[:, :, c].unsqueeze(1).to_broadcast([P, P, T]),
-                    op=ALU.mult,
+                    out=v1_grouped[chunk][:, m * P * T : (m + 1) * P * T].rearrange("p (n t) -> p n t", t=T),
+                    in0=mean_turned[chunk][m][:].rearrange("p t n -> p n t"),
+                    in1=minus_s[:, :, chunk].unsqueeze(1).to_broadcast([P, P, T]),
+                    op=MULT,
                 )
-            v1_group[c] = tile
 
-        def widen_hp(c):
-            tile = work.tile([P, T, H], BF16, name="hp_bf", tag="hp_bf")
+        def quantize_v1(chunk):
+            v1_mx[chunk] = quantize(v1_grouped[chunk], V, "v1")
+
+        def widen_hp(chunk):
+            hp_wide[chunk] = work.tile([P, T, H], BF16, name="hp_wide", tag="hp_wide")
             for t in range(T):
                 nc.scalar.activation(
-                    out=tile[:, t, :], in_=hp_raw[c][:, t, :].bitcast(FP8), func=ACT.Copy, scale=hp_sc[:, t, c : c + 1]
+                    out=hp_wide[chunk][:, t, :],
+                    in_=hp_raw[chunk][:, t, :].bitcast(FP8),
+                    func=COPY,
+                    scale=hp_factor[:, t, chunk : chunk + 1],
                 )
-            hp_bf[c] = tile
 
-        def group_v(c):
-            tile = work.tile([P, V * T], BF16, name="v_group", tag="v_group", align_bytes=64)
-            interleave(nc.scalar.copy, tile[:], v_raw[c][:], V)
-            v_group[c] = tile
+        def interleave_hp(chunk):
+            cut = LAST_HP_ON_SCALAR if chunk == CHUNKS - 1 else 0
+            hp_grouped[chunk] = grouped_tile("hp_grouped", H)
+            interleave(nc.scalar.copy, hp_grouped[chunk], hp_wide[chunk], 0, cut)
+            interleave(nc.vector.tensor_copy, hp_grouped[chunk], hp_wide[chunk], cut, H)
 
-        def group_h(copy, src, name):
-            tile = work.tile([P, H * T], BF16, name=name, tag=name, align_bytes=64)
-            interleave(copy, tile[:], src[:], H)
-            return tile
+        def quantize_hp(chunk):
+            hp_mx[chunk] = quantize(hp_grouped[chunk], H, "hp")
 
-        def add_passes(lhs, rhs):
-            code, scale = lhs
-            rcode, rscale = rhs
-            for m in range(M_TILES):
-                cols = slice(m * P, (m + 1) * P)
+        def interleave_v_on_scalar(chunk):
+            v_grouped[chunk] = grouped_tile("v_grouped", V)
+            interleave(nc.scalar.copy, v_grouped[chunk], v_raw[chunk], 0, V_ON_SCALAR)
+
+        def interleave_v_on_vector(chunk):
+            interleave(nc.vector.tensor_copy, v_grouped[chunk], v_raw[chunk], V_ON_SCALAR, V)
+
+        def quantize_v(chunk):
+            v_mx[chunk] = quantize(v_grouped[chunk], V, "v")
+
+        def hn_cuts(chunk):
+            scalar_end = LAST_HN_ON_SCALAR if chunk == CHUNKS - 1 else 0
+            return scalar_end, scalar_end + (HN_ON_GPSIMD if chunk > 0 else 0)
+
+        def interleave_hn_on_gpsimd(chunk):
+            hn_grouped[chunk] = grouped_tile("hn_grouped", H, bufs=1)
+            scalar_end, gpsimd_end = hn_cuts(chunk)
+            interleave(gpsimd_copy, hn_grouped[chunk], hn_raw[chunk], scalar_end, gpsimd_end)
+
+        def interleave_hn_on_scalar(chunk):
+            interleave(nc.scalar.copy, hn_grouped[chunk], hn_raw[chunk], 0, hn_cuts(chunk)[0])
+
+        def interleave_hn_on_vector(chunk):
+            interleave(nc.vector.tensor_copy, hn_grouped[chunk], hn_raw[chunk], hn_cuts(chunk)[1], H)
+
+        def quantize_hn(chunk):
+            hn_mx[chunk] = quantize(hn_grouped[chunk], H, "hn")
+
+        def add_phase(visible, hidden):
+            for m in range(V_TILES):
+                units = slice(m * P, (m + 1) * P)
                 nc.tensor.matmul_mx(
-                    out=acc[m][:],
-                    lhsT=code[:, cols].bitcast(FP8X4),
-                    lhsT_scale=scale[:, cols],
-                    rhs=rcode[:].bitcast(FP8X4),
-                    rhs_scale=rscale[:],
-                    start=(acc_passes[m] == 0),
-                    stop=(acc_passes[m] == 2 * CHUNKS - 1),
+                    out=total[m][:],
+                    lhsT=visible[0][:, units].bitcast(FP8X4),
+                    lhsT_scale=visible[1][:, units],
+                    rhs=hidden[0][:].bitcast(FP8X4),
+                    rhs_scale=hidden[1][:],
+                    start=(passes[m] == 0),
+                    stop=(passes[m] == 2 * CHUNKS - 1),
                 )
-                acc_passes[m] = acc_passes[m] + 1
+                passes[m] += 1
 
-        scale_bank = psum.tile([P, T, P], F32, name="back0", tag="back0")
+        factor_bank = psum.tile([P, T, P], F32, name="back0", tag="back0")
         for t in range(T):
-            nc.tensor.transpose(scale_bank[:, t, :], scale_rows[:, t::T], ident[:])
-        group_v(0)
-        nc.scalar.copy(out=hp_sc[:], in_=scale_bank[:, :, 0:CHUNKS])
-        hn_group[0] = group_h(nc.vector.tensor_copy, hn_raw[0], "hn_group")
-        vec_f32 = keep.tile([P, ROWS], F32, name="vec_f32")
-        nc.vector.tensor_copy(out=vec_f32[:], in_=vec_rows[:])
+            nc.tensor.transpose(factor_bank[:, t, :], scale_rows[:, t::T], ident[:])
+        nc.scalar.copy(out=hp_factor[:], in_=factor_bank[:, :, 0:CHUNKS])
+
+        vector_rows_f32 = keep.tile([P, ROWS], F32, name="vector_rows_f32")
+        nc.vector.tensor_copy(out=vector_rows_f32[:], in_=vector_rows[:])
         s_bank = psum.tile([P, T, P], F32, name="back1", tag="back1")
         for t in range(T):
-            nc.tensor.transpose(s_bank[:, t, :], vec_f32[:, t::T], ident[:])
-        b_bank = psum.tile([P, P], F32, name="field0", tag="field0")
-        nc.tensor.transpose(b_bank[:], vec_f32[:, 0:P], ident[:])
-        nc.vector.tensor_scalar(out=neg_s[:], in0=s_bank[:, :, 0:CHUNKS], scalar1=-1.0, scalar2=None, op0=ALU.mult)
-        nc.vector.tensor_copy(out=b_col[:], in_=b_bank[:, 32 : 32 + M_TILES])
+            nc.tensor.transpose(s_bank[:, t, :], vector_rows_f32[:, t::T], ident[:])
+        b_bank = psum.tile([P, P], F32, name="field1", tag="field1")
+        nc.tensor.transpose(b_bank[:], vector_rows_f32[:, 0:P], ident[:])
+
+        interleave_hn_on_gpsimd(0)
+        interleave_hn_on_vector(0)
         widen_hp(0)
+        interleave_v_on_scalar(0)
+        interleave_v_on_vector(0)
+
+        nc.scalar.activation(out=minus_s[:], in_=s_bank[:, :, 0:CHUNKS], func=COPY, scale=-1.0)
+        nc.scalar.copy(out=bias[:], in_=b_bank[:, B_ROW : B_ROW + V_TILES])
+
+        w_bank = turn_two_rows(w_raw[:].rearrange("p m k -> p (m k)").bitcast(F32), "field0")
+        w_grouped = keep.tile([P, V * T], BF16, name="w_grouped", align_bytes=64)
+        empty_turned(nc.vector.tensor_copy, w_bank, w_grouped[:])
+        nc.vector.quantize_mx(out=w_codes[:].bitcast(FP8X4), scales=w_scales[:], in_=w_grouped[:])
         turn_hf(0)
 
-        for step in range(STEPS + 1):
-            hn_now = chunk_of_step(step, HN_GAPS)
-            hp_now = chunk_of_step(step, HP_GAPS)
-            hp_next = chunk_of_step(step + 1, HP_GAPS)
-            hp_prev = chunk_of_step(step - 1, HP_GAPS)
-            hn_next = chunk_of_step(step + 1, HN_GAPS)
+        for step in range(CHUNKS + 2):
+            now, following, before = step, step + 1, step - 1
+            hn_now, hn_following = hn_chunk(step), hn_chunk(step + 1)
 
-            for ahead in range(LEAD + 1):
-                c = chunk_of_step(step + ahead + 1, HP_GAPS)
-                if c is not None and c not in hp_raw:
-                    load_hp(c)
-                    load_v(c)
-                c = step + ahead + 1
-                if c < CHUNKS and c not in hf_raw:
-                    load_hf(c)
-                c = chunk_of_step(step + ahead + 1, HN_GAPS)
-                if c is not None and c not in hn_raw:
-                    load_hn(c)
+            if step + LOADS_AHEAD < CHUNKS:
+                load_hp(step + LOADS_AHEAD)
+                load_v(step + LOADS_AHEAD)
+                load_hf(step + LOADS_AHEAD)
+            if hn_chunk(step + LOADS_AHEAD) is not None:
+                load_hn(hn_chunk(step + LOADS_AHEAD))
 
-            if 0 <= step - 1 < CHUNKS:
-                fields(step - 1)
-            if hp_prev is not None:
-                add_passes(v_codes[hp_prev], hp_codes[hp_prev])
-
-            if step < CHUNKS:
-                empty_hf(step)
-            if 0 <= step - 1 < CHUNKS:
-                means(step - 1)
-
-            if 0 <= step - 2 < CHUNKS:
-                weigh_means(step - 2)
-
-            if step + 1 < CHUNKS:
-                turn_hf(step + 1)
-            if 0 <= step - 3 < CHUNKS:
-                add_passes(v1_codes[step - 3], hn_codes[step - 3])
-            if 0 <= step - 1 < CHUNKS:
-                turn_means(step - 1)
-
-            if hp_next is not None:
-                widen_hp(hp_next)
-                group_v(hp_next)
-            if hn_next == CHUNKS - 1:
-                hn_group[hn_next] = group_h(nc.scalar.copy, hn_raw[hn_next], "hn_group")
-
-            if hp_now is not None:
-                hp_group[hp_now] = group_h(nc.vector.tensor_copy, hp_bf[hp_now], "hp_group")
-            if 0 <= step - 2 < CHUNKS:
-                v1_codes[step - 2] = quantize(v1_group[step - 2], V, "v1")
+            if now < CHUNKS:
+                empty_hf(now)
+                quantize_v(now)
+            if following < CHUNKS:
+                interleave_v_on_scalar(following)
+            if 0 <= before < CHUNKS:
+                turn_means(before)
+                add_phase(v_mx[before], hp_mx[before])
+            if now < CHUNKS:
+                interleave_hp(now)
+            if following < CHUNKS:
+                turn_hf(following)
+                widen_hp(following)
+            if now < CHUNKS:
+                quantize_hf(now)
+                compute_fields(now)
+            if following < CHUNKS:
+                interleave_v_on_vector(following)
             if hn_now is not None:
-                hn_codes[hn_now] = quantize(hn_group[hn_now], H, "hn")
-            if hp_now is not None:
-                v_codes[hp_now] = quantize(v_group[hp_now], V, "v")
-                hp_codes[hp_now] = quantize(hp_group[hp_now], H, "hp")
-            if step == 0:
-                w_bank = turn_words(w_raw[:].rearrange("p m k -> p (m k)").bitcast(F32), "back0")
-                w_group = keep.tile([P, V * T], BF16, name="w_group", align_bytes=64)
-                empty_turned(nc.vector.tensor_copy, w_bank, w_group[:])
-                nc.vector.quantize_mx(out=w_codes[:].bitcast(FP8X4), scales=w_scales[:], in_=w_group[:])
-            if step < CHUNKS:
-                hf_codes[step] = quantize(hf_turned[step], ROWS, "hf")
-            if hn_next is not None and hn_next < CHUNKS - 1:
-                hn_group[hn_next] = group_h(nc.vector.tensor_copy, hn_raw[hn_next], "hn_group")
+                quantize_hn(hn_now)
+            if hn_following is not None:
+                interleave_hn_on_gpsimd(hn_following)
+            if 0 <= before < CHUNKS:
+                weigh_means(before)
+            if step >= 2:
+                add_phase(v1_mx[step - 2], hn_mx[step - 2])
+            if now < CHUNKS:
+                quantize_hp(now)
+            if hn_following is not None:
+                interleave_hn_on_scalar(hn_following)
+                interleave_hn_on_vector(hn_following)
+            if 0 <= before < CHUNKS:
+                quantize_v1(before)
+            if now < CHUNKS:
+                compute_means(now)
 
-        for m in range(M_TILES):
+        for m in range(V_TILES):
             result = keep.tile([P, H], F32, name="result%d" % m)
             if m == 0:
-                nc.scalar.activation(out=result[:], in_=acc[m][:], func=ACT.Copy, scale=B ** -0.5)
+                nc.scalar.activation(out=result[:], in_=total[m][:], func=COPY, scale=B**-0.5)
             else:
-                nc.vector.tensor_scalar(out=result[:], in0=acc[m][:], scalar1=B ** -0.5, scalar2=None, op0=ALU.mult)
+                nc.vector.tensor_scalar(out=result[:], in0=total[m][:], scalar1=B**-0.5, scalar2=None, op0=MULT)
             nc.sync.dma_start(out=out[m * P : (m + 1) * P, :], in_=result[:])

@@ -23,19 +23,18 @@ V_TILES = V // P
 B_ROW = 32
 
 LOADS_AHEAD = 3
-HN_PAUSE = 12
+HN_PAUSES = (1,)
+HP_PAUSES = (7, 12)
 
-V_ON_SCALAR = 224
-HN_ON_GPSIMD = 176
-LAST_HN_ON_SCALAR = 320
-LAST_HP_ON_SCALAR = 256
+HN_ON_GPSIMD = 160
+LAST_HP_ON_SCALAR = 192
 
 FLOPS = 3 * 2 * B * V * H
 
 
-def hn_chunk(step):
-    chunk = step if step < HN_PAUSE else step - 1
-    return chunk if step != HN_PAUSE and chunk < CHUNKS else None
+def chunk_at(step, pauses):
+    chunk = step - sum(1 for pause in pauses if pause < step)
+    return chunk if 0 <= chunk < CHUNKS and step not in pauses else None
 
 
 def tile_persistentmeanfieldisingrbmgradient_t_kernel(tc, v, hp_bytes, hp_scale, hf, hn, w, b, s, out):
@@ -83,19 +82,18 @@ def tile_persistentmeanfieldisingrbmgradient_t_kernel(tc, v, hp_bytes, hp_scale,
         nc.scalar.dma_start(out=vector_rows[B_ROW : B_ROW + V_TILES, 0:P], in_=b.rearrange("(m x) -> m x", x=P))
         w_raw = keep.tile([P, V_TILES, H], BF16, name="w_raw")
 
-        load_hp(0)
         load_v(0)
+        load_hp(0)
         load_hn(0)
         nc.sync.dma_start(out=w_raw[:], in_=w.rearrange("(m p) k -> p m k", p=P))
         load_hf(0)
-        load_hf(1)
         load_v(1)
+        load_hn(1)
         load_hp(1)
         load_hf(2)
-        load_hn(1)
+        load_hf(1)
         load_hp(2)
         load_v(2)
-        load_hn(2)
 
         hp_factor = keep.tile([P, T, CHUNKS], F32, name="hp_factor")
         minus_s = keep.tile([P, T, CHUNKS], F32, name="minus_s")
@@ -216,30 +214,19 @@ def tile_persistentmeanfieldisingrbmgradient_t_kernel(tc, v, hp_bytes, hp_scale,
         def quantize_hp(chunk):
             hp_mx[chunk] = quantize(hp_grouped[chunk], H, "hp")
 
-        def interleave_v_on_scalar(chunk):
+        def interleave_v(chunk):
             v_grouped[chunk] = grouped_tile("v_grouped", V)
-            interleave(nc.scalar.copy, v_grouped[chunk], v_raw[chunk], 0, V_ON_SCALAR)
-
-        def interleave_v_on_vector(chunk):
-            interleave(nc.vector.tensor_copy, v_grouped[chunk], v_raw[chunk], V_ON_SCALAR, V)
+            interleave(nc.scalar.copy, v_grouped[chunk], v_raw[chunk], 0, V)
 
         def quantize_v(chunk):
             v_mx[chunk] = quantize(v_grouped[chunk], V, "v")
 
-        def hn_cuts(chunk):
-            scalar_end = LAST_HN_ON_SCALAR if chunk == CHUNKS - 1 else 0
-            return scalar_end, scalar_end + (HN_ON_GPSIMD if chunk > 0 else 0)
-
         def interleave_hn_on_gpsimd(chunk):
             hn_grouped[chunk] = grouped_tile("hn_grouped", H, bufs=1)
-            scalar_end, gpsimd_end = hn_cuts(chunk)
-            interleave(gpsimd_copy, hn_grouped[chunk], hn_raw[chunk], scalar_end, gpsimd_end)
-
-        def interleave_hn_on_scalar(chunk):
-            interleave(nc.scalar.copy, hn_grouped[chunk], hn_raw[chunk], 0, hn_cuts(chunk)[0])
+            interleave(gpsimd_copy, hn_grouped[chunk], hn_raw[chunk], 0, HN_ON_GPSIMD if chunk > 0 else 0)
 
         def interleave_hn_on_vector(chunk):
-            interleave(nc.vector.tensor_copy, hn_grouped[chunk], hn_raw[chunk], hn_cuts(chunk)[1], H)
+            interleave(nc.vector.tensor_copy, hn_grouped[chunk], hn_raw[chunk], HN_ON_GPSIMD if chunk > 0 else 0, H)
 
         def quantize_hn(chunk):
             hn_mx[chunk] = quantize(hn_grouped[chunk], H, "hn")
@@ -258,10 +245,11 @@ def tile_persistentmeanfieldisingrbmgradient_t_kernel(tc, v, hp_bytes, hp_scale,
                 )
                 passes[m] += 1
 
-        factor_bank = psum.tile([P, T, P], F32, name="back0", tag="back0")
-        for t in range(T):
-            nc.tensor.transpose(factor_bank[:, t, :], scale_rows[:, t::T], ident[:])
-        nc.scalar.copy(out=hp_factor[:], in_=factor_bank[:, :, 0:CHUNKS])
+        def add_positive(chunk):
+            add_phase(v_mx[chunk], hp_mx[chunk])
+
+        def add_negative(chunk):
+            add_phase(v1_mx[chunk], hn_mx[chunk])
 
         vector_rows_f32 = keep.tile([P, ROWS], F32, name="vector_rows_f32")
         nc.vector.tensor_copy(out=vector_rows_f32[:], in_=vector_rows[:])
@@ -273,65 +261,53 @@ def tile_persistentmeanfieldisingrbmgradient_t_kernel(tc, v, hp_bytes, hp_scale,
 
         interleave_hn_on_gpsimd(0)
         interleave_hn_on_vector(0)
-        widen_hp(0)
-        interleave_v_on_scalar(0)
-        interleave_v_on_vector(0)
-
+        interleave_v(0)
         nc.scalar.activation(out=minus_s[:], in_=s_bank[:, :, 0:CHUNKS], func=COPY, scale=-1.0)
         nc.scalar.copy(out=bias[:], in_=b_bank[:, B_ROW : B_ROW + V_TILES])
+
+        factor_bank = psum.tile([P, T, P], F32, name="back0", tag="back0")
+        for t in range(T):
+            nc.tensor.transpose(factor_bank[:, t, :], scale_rows[:, t::T], ident[:])
+        nc.scalar.copy(out=hp_factor[:], in_=factor_bank[:, :, 0:CHUNKS])
 
         w_bank = turn_two_rows(w_raw[:].rearrange("p m k -> p (m k)").bitcast(F32), "field0")
         w_grouped = keep.tile([P, V * T], BF16, name="w_grouped", align_bytes=64)
         empty_turned(nc.vector.tensor_copy, w_bank, w_grouped[:])
         nc.vector.quantize_mx(out=w_codes[:].bitcast(FP8X4), scales=w_scales[:], in_=w_grouped[:])
         turn_hf(0)
+        widen_hp(0)
 
-        for step in range(CHUNKS + 2):
-            now, following, before = step, step + 1, step - 1
-            hn_now, hn_following = hn_chunk(step), hn_chunk(step + 1)
+        def run(stage, chunk):
+            if chunk is not None and 0 <= chunk < CHUNKS:
+                stage(chunk)
 
-            if step + LOADS_AHEAD < CHUNKS:
-                load_hp(step + LOADS_AHEAD)
-                load_v(step + LOADS_AHEAD)
-                load_hf(step + LOADS_AHEAD)
-            if hn_chunk(step + LOADS_AHEAD) is not None:
-                load_hn(hn_chunk(step + LOADS_AHEAD))
+        for step in range(CHUNKS + 4):
+            hn_now, hn_next = chunk_at(step, HN_PAUSES), chunk_at(step + 1, HN_PAUSES)
+            hp_now, hp_next = chunk_at(step, HP_PAUSES), chunk_at(step + 1, HP_PAUSES)
 
-            if now < CHUNKS:
-                empty_hf(now)
-                quantize_v(now)
-            if following < CHUNKS:
-                interleave_v_on_scalar(following)
-            if 0 <= before < CHUNKS:
-                turn_means(before)
-                add_phase(v_mx[before], hp_mx[before])
-            if now < CHUNKS:
-                interleave_hp(now)
-            if following < CHUNKS:
-                turn_hf(following)
-                widen_hp(following)
-            if now < CHUNKS:
-                quantize_hf(now)
-                compute_fields(now)
-            if following < CHUNKS:
-                interleave_v_on_vector(following)
-            if hn_now is not None:
-                quantize_hn(hn_now)
-            if hn_following is not None:
-                interleave_hn_on_gpsimd(hn_following)
-            if 0 <= before < CHUNKS:
-                weigh_means(before)
-            if step >= 2:
-                add_phase(v1_mx[step - 2], hn_mx[step - 2])
-            if now < CHUNKS:
-                quantize_hp(now)
-            if hn_following is not None:
-                interleave_hn_on_scalar(hn_following)
-                interleave_hn_on_vector(hn_following)
-            if 0 <= before < CHUNKS:
-                quantize_v1(before)
-            if now < CHUNKS:
-                compute_means(now)
+            run(load_hp, chunk_at(step + LOADS_AHEAD, HP_PAUSES))
+            run(load_v, chunk_at(step + LOADS_AHEAD, HP_PAUSES))
+            run(load_hf, step + LOADS_AHEAD)
+            run(load_hn, chunk_at(step + LOADS_AHEAD, HN_PAUSES))
+
+            run(compute_fields, step - 1)
+            run(quantize_hn, hn_now)
+            run(add_positive, chunk_at(step - 2, HP_PAUSES))
+            run(empty_hf, step)
+            run(interleave_hn_on_gpsimd, hn_next)
+            run(interleave_v, hp_next)
+            run(weigh_means, step - 2)
+            run(turn_hf, step + 1)
+            run(add_negative, step - 3)
+            run(interleave_hn_on_vector, hn_next)
+            run(quantize_v, hp_now)
+            run(compute_means, step - 1)
+            run(interleave_hp, hp_now)
+            run(turn_means, step - 1)
+            run(quantize_hf, step)
+            run(widen_hp, hp_next)
+            run(quantize_v1, step - 2)
+            run(quantize_hp, hp_now)
 
         for m in range(V_TILES):
             result = keep.tile([P, H], F32, name="result%d" % m)

from contextlib import ExitStack

import concourse.mybir as mybir
from concourse.masks import make_identity

F32 = mybir.dt.float32
BF16 = mybir.dt.bfloat16
U32 = mybir.dt.uint32
U8 = mybir.dt.uint8
FP8 = mybir.dt.float8_e4m3fn
FP8X4 = mybir.dt.float8_e4m3fn_x4
TANH = mybir.ActivationFunctionType.Tanh
COPY = mybir.ActivationFunctionType.Copy
MULT = mybir.AluOpType.mult
ADD = mybir.AluOpType.add

B, V, H = 8192, 256, 512
P = 128
T = 4
ROWS = P * T
CHUNKS = B // ROWS
V_TILES = V // P
B_ROW = 32

LOADS_AHEAD = 3
HN_PAUSES = (1,)
HP_PAUSES = (7, 12)

HN_ON_GPSIMD = 160
LAST_HP_ON_SCALAR = 192

FLOPS = 3 * 2 * B * V * H


def chunk_at(step, pauses):
    chunk = step - sum(1 for pause in pauses if pause < step)
    return chunk if 0 <= chunk < CHUNKS and step not in pauses else None


def tile_persistentmeanfieldisingrbmgradient_t_kernel(tc, v, hp_bytes, hp_scale, hf, hn, w, b, s, out):
    nc = tc.nc

    with ExitStack() as ctx:
        keep = ctx.enter_context(tc.tile_pool(name="keep", bufs=1))
        raw = ctx.enter_context(tc.tile_pool(name="raw", bufs=4))
        work = ctx.enter_context(tc.tile_pool(name="work", bufs=2))
        codes = ctx.enter_context(tc.tile_pool(name="codes", bufs=3))
        psum = ctx.enter_context(tc.psum_pool(name="psum", bufs=1))
        ctx.enter_context(tc.manual_schedule())

        warm = keep.tile([P, 1], F32, name="warm")
        nc.vector.memset(warm[:], 0.0)
        nc.scalar.activation(out=warm[:], in_=warm[:], func=TANH)
        scale_rows = keep.tile([P, ROWS], F32, name="scale_rows")
        nc.vector.memset(scale_rows[:], 0.0)
        vector_rows = keep.tile([P, ROWS], BF16, name="vector_rows")
        nc.gpsimd.memset(vector_rows[:], 0.0)
        ident = keep.tile([P, P], F32, name="ident")
        make_identity(nc, ident[:])

        hp_raw, v_raw, hn_raw, hf_raw = {}, {}, {}, {}

        def load(store, name, source, chunk, dtype):
            rows = source.rearrange("(g p t) n -> g p t n", p=P, t=T)[chunk]
            store[chunk] = raw.tile([P, T, source.shape[1]], dtype, name=name, tag=name)
            nc.sync.dma_start(out=store[chunk][:], in_=rows)

        def load_hp(chunk):
            load(hp_raw, "hp_raw", hp_bytes, chunk, U8)

        def load_v(chunk):
            load(v_raw, "v_raw", v, chunk, BF16)

        def load_hn(chunk):
            load(hn_raw, "hn_raw", hn, chunk, BF16)

        def load_hf(chunk):
            load(hf_raw, "hf_raw", hf, chunk, BF16)

        nc.scalar.dma_start(out=scale_rows[0:CHUNKS, :], in_=hp_scale.rearrange("(g x) o -> g (x o)", x=ROWS))
        nc.scalar.dma_start(out=vector_rows[0:CHUNKS, :], in_=s.rearrange("(g x) -> g x", x=ROWS))
        nc.scalar.dma_start(out=vector_rows[B_ROW : B_ROW + V_TILES, 0:P], in_=b.rearrange("(m x) -> m x", x=P))
        w_raw = keep.tile([P, V_TILES, H], BF16, name="w_raw")

        load_v(0)
        load_hp(0)
        load_hn(0)
        nc.sync.dma_start(out=w_raw[:], in_=w.rearrange("(m p) k -> p m k", p=P))
        load_hf(0)
        load_v(1)
        load_hn(1)
        load_hp(1)
        load_hf(2)
        load_hf(1)
        load_hp(2)
        load_v(2)

        hp_factor = keep.tile([P, T, CHUNKS], F32, name="hp_factor")
        minus_s = keep.tile([P, T, CHUNKS], F32, name="minus_s")
        bias = keep.tile([P, V_TILES], F32, name="bias")
        w_codes = keep.tile([P, V], U32, name="w_codes", align_bytes=64)
        w_scales = keep.tile([P, V], U8, name="w_scales", align_bytes=64)
        total = [psum.tile([P, H], F32, name="total%d" % m, tag="total%d" % m) for m in range(V_TILES)]
        passes = [0, 0]

        hf_turned, hf_grouped, hf_mx, field, mean, mean_turned, v1_grouped, v1_mx = {}, {}, {}, {}, {}, {}, {}, {}
        hp_wide, hp_grouped, hp_mx, v_grouped, v_mx, hn_grouped, hn_mx = {}, {}, {}, {}, {}, {}, {}

        def gpsimd_copy(out, in_):
            nc.gpsimd.tensor_scalar(out=out, in0=in_, scalar1=1.0, scalar2=0.0, op0=MULT, op1=ADD)

        def interleave(copy, grouped, source, start, stop):
            if start < stop:
                copy(
                    out=grouped[:, start * T : stop * T].rearrange("p (c i t) -> p c t i", i=4, t=T),
                    in_=source[:, :, start:stop].rearrange("p t (c i) -> p c t i", i=4),
                )

        def grouped_tile(name, columns, bufs=2):
            return work.tile([P, columns * T], BF16, name=name, tag=name, align_bytes=64, bufs=bufs)

        def quantize(grouped, columns, name):
            code = codes.tile([P, columns], U32, name=name + "_codes", tag=name + "_codes", align_bytes=64)
            scale = codes.tile([P, columns], U8, name=name + "_scales", tag=name + "_scales", align_bytes=64)
            nc.vector.quantize_mx(out=code[:].bitcast(FP8X4), scales=scale[:], in_=grouped[:])
            return code, scale

        def turn_two_rows(words, bank_name):
            bank = psum.tile([P, 2, 2, P], F32, name=bank_name, tag=bank_name)
            for r in range(2):
                for u in range(2):
                    nc.tensor.transpose(bank[:, r, u, :], words[:, 256 * r + u : 256 * (r + 1) : 2], ident[:])
            return bank

        def empty_turned(copy, bank, grouped):
            copy(
                out=grouped.bitcast(F32).rearrange("p (r c u) -> p r c u", r=2, u=2),
                in_=bank[:].rearrange("p r u c -> p r c u"),
            )

        def turn_hf(chunk):
            words = hf_raw[chunk][:].rearrange("p t k -> p (t k)").bitcast(F32)
            hf_turned[chunk] = [turn_two_rows(words[:, 512 * i : 512 * (i + 1)], "turned%d" % i) for i in range(2)]

        def empty_hf(chunk):
            hf_grouped[chunk] = grouped_tile("hf_grouped", ROWS)
            for i in range(2):
                empty_turned(nc.scalar.copy, hf_turned[chunk][i], hf_grouped[chunk][:, 1024 * i : 1024 * (i + 1)])

        def quantize_hf(chunk):
            hf_mx[chunk] = quantize(hf_grouped[chunk], ROWS, "hf")

        def compute_fields(chunk):
            code, scale = hf_mx[chunk]
            field[chunk] = []
            for m in range(V_TILES):
                units = slice(m * P, (m + 1) * P)
                bank = psum.tile([P, ROWS], F32, name="field%d" % m, tag="field%d" % m)
                nc.tensor.matmul_mx(
                    out=bank[:],
                    lhsT=w_codes[:, units].bitcast(FP8X4),
                    lhsT_scale=w_scales[:, units],
                    rhs=code[:].bitcast(FP8X4),
                    rhs_scale=scale[:],
                    start=True,
                    stop=True,
                )
                field[chunk].append(bank)

        def compute_means(chunk):
            mean[chunk] = work.tile([P, V_TILES, ROWS], F32, name="mean", tag="mean")
            for m in range(V_TILES):
                nc.scalar.activation(
                    out=mean[chunk][:, m, :], in_=field[chunk][m][:], func=TANH, bias=bias[:, m : m + 1], scale=1.0
                )

        def turn_means(chunk):
            mean_turned[chunk] = []
            for m in range(V_TILES):
                bank = psum.tile([P, T, P], F32, name="back%d" % m, tag="back%d" % m)
                for t in range(T):
                    nc.tensor.transpose(bank[:, t, :], mean[chunk][:, m, t * P : (t + 1) * P], ident[:])
                mean_turned[chunk].append(bank)

        def weigh_means(chunk):
            v1_grouped[chunk] = grouped_tile("v1_grouped", V)
            for m in range(V_TILES):
                nc.vector.tensor_tensor(
                    out=v1_grouped[chunk][:, m * P * T : (m + 1) * P * T].rearrange("p (n t) -> p n t", t=T),
                    in0=mean_turned[chunk][m][:].rearrange("p t n -> p n t"),
                    in1=minus_s[:, :, chunk].unsqueeze(1).to_broadcast([P, P, T]),
                    op=MULT,
                )

        def quantize_v1(chunk):
            v1_mx[chunk] = quantize(v1_grouped[chunk], V, "v1")

        def widen_hp(chunk):
            hp_wide[chunk] = work.tile([P, T, H], BF16, name="hp_wide", tag="hp_wide")
            for t in range(T):
                nc.scalar.activation(
                    out=hp_wide[chunk][:, t, :],
                    in_=hp_raw[chunk][:, t, :].bitcast(FP8),
                    func=COPY,
                    scale=hp_factor[:, t, chunk : chunk + 1],
                )

        def interleave_hp(chunk):
            cut = LAST_HP_ON_SCALAR if chunk == CHUNKS - 1 else 0
            hp_grouped[chunk] = grouped_tile("hp_grouped", H)
            interleave(nc.scalar.copy, hp_grouped[chunk], hp_wide[chunk], 0, cut)
            interleave(nc.vector.tensor_copy, hp_grouped[chunk], hp_wide[chunk], cut, H)

        def quantize_hp(chunk):
            hp_mx[chunk] = quantize(hp_grouped[chunk], H, "hp")

        def interleave_v(chunk):
            v_grouped[chunk] = grouped_tile("v_grouped", V)
            interleave(nc.scalar.copy, v_grouped[chunk], v_raw[chunk], 0, V)

        def quantize_v(chunk):
            v_mx[chunk] = quantize(v_grouped[chunk], V, "v")

        def interleave_hn_on_gpsimd(chunk):
            hn_grouped[chunk] = grouped_tile("hn_grouped", H, bufs=1)
            interleave(gpsimd_copy, hn_grouped[chunk], hn_raw[chunk], 0, HN_ON_GPSIMD if chunk > 0 else 0)

        def interleave_hn_on_vector(chunk):
            interleave(nc.vector.tensor_copy, hn_grouped[chunk], hn_raw[chunk], HN_ON_GPSIMD if chunk > 0 else 0, H)

        def quantize_hn(chunk):
            hn_mx[chunk] = quantize(hn_grouped[chunk], H, "hn")

        def add_phase(visible, hidden):
            for m in range(V_TILES):
                units = slice(m * P, (m + 1) * P)
                nc.tensor.matmul_mx(
                    out=total[m][:],
                    lhsT=visible[0][:, units].bitcast(FP8X4),
                    lhsT_scale=visible[1][:, units],
                    rhs=hidden[0][:].bitcast(FP8X4),
                    rhs_scale=hidden[1][:],
                    start=(passes[m] == 0),
                    stop=(passes[m] == 2 * CHUNKS - 1),
                )
                passes[m] += 1

        def add_positive(chunk):
            add_phase(v_mx[chunk], hp_mx[chunk])

        def add_negative(chunk):
            add_phase(v1_mx[chunk], hn_mx[chunk])

        vector_rows_f32 = keep.tile([P, ROWS], F32, name="vector_rows_f32")
        nc.vector.tensor_copy(out=vector_rows_f32[:], in_=vector_rows[:])
        s_bank = psum.tile([P, T, P], F32, name="back1", tag="back1")
        for t in range(T):
            nc.tensor.transpose(s_bank[:, t, :], vector_rows_f32[:, t::T], ident[:])
        b_bank = psum.tile([P, P], F32, name="field1", tag="field1")
        nc.tensor.transpose(b_bank[:], vector_rows_f32[:, 0:P], ident[:])

        interleave_hn_on_gpsimd(0)
        interleave_hn_on_vector(0)
        interleave_v(0)
        nc.scalar.activation(out=minus_s[:], in_=s_bank[:, :, 0:CHUNKS], func=COPY, scale=-1.0)
        nc.scalar.copy(out=bias[:], in_=b_bank[:, B_ROW : B_ROW + V_TILES])

        factor_bank = psum.tile([P, T, P], F32, name="back0", tag="back0")
        for t in range(T):
            nc.tensor.transpose(factor_bank[:, t, :], scale_rows[:, t::T], ident[:])
        nc.scalar.copy(out=hp_factor[:], in_=factor_bank[:, :, 0:CHUNKS])

        w_bank = turn_two_rows(w_raw[:].rearrange("p m k -> p (m k)").bitcast(F32), "field0")
        w_grouped = keep.tile([P, V * T], BF16, name="w_grouped", align_bytes=64)
        empty_turned(nc.vector.tensor_copy, w_bank, w_grouped[:])
        nc.vector.quantize_mx(out=w_codes[:].bitcast(FP8X4), scales=w_scales[:], in_=w_grouped[:])
        turn_hf(0)
        widen_hp(0)

        def run(stage, chunk):
            if chunk is not None and 0 <= chunk < CHUNKS:
                stage(chunk)

        for step in range(CHUNKS + 4):
            hn_now, hn_next = chunk_at(step, HN_PAUSES), chunk_at(step + 1, HN_PAUSES)
            hp_now, hp_next = chunk_at(step, HP_PAUSES), chunk_at(step + 1, HP_PAUSES)

            run(load_hp, chunk_at(step + LOADS_AHEAD, HP_PAUSES))
            run(load_v, chunk_at(step + LOADS_AHEAD, HP_PAUSES))
            run(load_hf, step + LOADS_AHEAD)
            run(load_hn, chunk_at(step + LOADS_AHEAD, HN_PAUSES))

            run(compute_fields, step - 1)
            run(quantize_hn, hn_now)
            run(add_positive, chunk_at(step - 2, HP_PAUSES))
            run(empty_hf, step)
            run(interleave_hn_on_gpsimd, hn_next)
            run(interleave_v, hp_next)
            run(weigh_means, step - 2)
            run(turn_hf, step + 1)
            run(add_negative, step - 3)
            run(interleave_hn_on_vector, hn_next)
            run(quantize_v, hp_now)
            run(compute_means, step - 1)
            run(interleave_hp, hp_now)
            run(turn_means, step - 1)
            run(quantize_hf, step)
            run(widen_hp, hp_next)
            run(quantize_v1, step - 2)
            run(quantize_hp, hp_now)

        for m in range(V_TILES):
            result = keep.tile([P, H], F32, name="result%d" % m)
            if m == 0:
                nc.scalar.activation(out=result[:], in_=total[m][:], func=COPY, scale=B**-0.5)
            else:
                nc.vector.tensor_scalar(out=result[:], in0=total[m][:], scalar1=B**-0.5, scalar2=None, op0=MULT)
            nc.sync.dma_start(out=out[m * P : (m + 1) * P, :], in_=result[:])
